import numpy as np, ml_dtypes
CORES = [36,38,116,118,124,126,164,166,244,246,252,254]
N = 12
import mx_ref
NC, G, MB = 256, 4, 1
C = np.float32(0.043)
BF = ml_dtypes.bfloat16
def cut(t, i, w=512):
    return t[:, w * i:w * i + w]
def tile(rs):
    return np.stack(rs, axis=2).reshape(128, -1).astype(BF)
def layer(w, X):
    out = []
    for i in range(G):
        for t in range(len(X)):
            p = mx_ref.matmul(mx_ref.quantize(cut(w, len(X) * i + t)), X[t])
            z = p if t == 0 else z + p
        out.append(z)
    return out
def act(Z):
    return [np.maximum(z, 0) * C for z in Z]
def setup_inputs(rng):
    def f(*shape):
        return mx_ref.flush((rng.standard_normal(shape, dtype=np.float32) * np.exp2(rng.integers(-2, 3, shape[:-1] + (1,)))).astype(BF))
    return {"x": f(N, 128, MB * 4 * NC), "w": f(N, 128, G * 512)}
def setup_inputs_blocks(rng):
    d = setup_inputs(rng)
    for k in ("x",): d[k] = mx_ref.spread(d[k], rng, 4)
    for k in ("w",): d[k] = mx_ref.spread(d[k], rng, 1)
    return d
def setup_inputs_wide(rng):
    d = setup_inputs(rng)
    for k in ("x",): d[k] = mx_ref.flush((d[k].astype(np.float32) * np.exp2(rng.integers(-8, 9, (N, 1, 1))).astype(np.float32)).astype(BF))
    return d
def setup_inputs_zeros(rng):
    d = setup_inputs(rng); v = d["x"].reshape(N, 128, -1, 4).copy()
    v[np.broadcast_to((rng.random((N, 1, v.shape[2], 1)) < 0.33), v.shape)] = 0
    d["x"] = v.reshape(d["x"].shape)
    return d
def reference(x, w):
    y = np.full((N, 128, MB * G * NC), np.nan, np.float32)
    for m in range(MB):
        a = mx_ref.quantize(cut(x[N - 1], m, 4 * NC))
        for s in range(N - 1):
            a = mx_ref.quantize(tile(act(layer(w[s], [a]))))
        Z = layer(w[N - 1], [a])
        for i in range(G):
            y[N - 1][:, NC * (G * m + i):NC * (G * m + i) + NC] = Z[i]
    return {"y": y}

from concourse.mybir import dt, AluOpType, ActivationFunctionType

NC = 256
CW = 128
NP = NC // CW
G = 4
SCALE = 0.043
BANK = 512
ENG_ON = 8
ENG_OFF = 8

SCRATCH = {
    "wt": ("sbuf", [128, G * 512], "bfloat16"),
    "wq": ("sbuf", [128, G * 128], "float8_e4m3fn_x4"),
    "ws": ("sbuf", [128, G * 128], "uint8"),
    "t": ("sbuf", [128, 4 * NC], "bfloat16"),
    "hq": ("sbuf", [128, NC], "float8_e4m3fn_x4"),
    "hs": ("sbuf", [128, NC], "uint8"),
    "aq": ("sbuf", [128, NC], "float8_e4m3fn_x4"),
    "asc": ("sbuf", [128, NC], "uint8"),
    "ps": ("psum", [128, NP * G * BANK], "float32"),
    "yt": ("sbuf", [128, G * NC], "float32"),
}
SEMAPHORES = (["wl0", "wl1", "xl0", "xl1", "wq0", "wq1", "arr0", "arr1", "act0", "act1", "q0", "q1", "sent", "st0", "st1"]
              + ["mm%d" % j for j in range(NP * G)] + ["cp%d" % j for j in range(NP * G)])


def _engines(topo, src, dst):
    allowed = topo.mask(src, dst)
    bits = [b for b in range(allowed.bit_length()) if (allowed >> b) & 1]
    on_chip = topo.host(src) == topo.host(dst) and topo.chip(src) == topo.chip(dst)
    k = min(ENG_ON if on_chip else ENG_OFF, len(bits))
    step = len(bits) // k
    mask = 0
    for b in bits[0:k * step:step]:
        mask |= 1 << b
    return mask, k


def rank_program(g, core, T, topo):
    rank = T.rank_of(core)
    if rank is None:
        return
    n = len(T.cores)
    last = rank == n - 1
    S = T.sem
    nxt, prv = T.cores[(rank + 1) % n], T.cores[(rank - 1) % n]
    assert topo.may_write(core, nxt)
    rid, pid = topo.addr(nxt, core)
    mask, k_out = _engines(topo, core, nxt)
    k_in = _engines(topo, prv, core)[1]
    ldq = (g.sync, g.scalar)

    if last:
        for c in range(NP):
            ldq[c].dma_start(T.t[:, 4 * CW * c:4 * CW * (c + 1)], T.x[:, 4 * CW * c:4 * CW * (c + 1)]).then_inc(S["xl%d" % c], 16)
    for h in range(2):
        ldq[h].dma_start(T.wt[:, 1024 * h:1024 * (h + 1)], T.w[:, 1024 * h:1024 * (h + 1)]).then_inc(S["wl%d" % h], 16)

    if last:
        for c in range(NP):
            g.vector.wait_ge(S["xl%d" % c], 16)
            g.vector.quantize_mx(T.hq[:, CW * c:CW * (c + 1)], T.hs[:, CW * c:CW * (c + 1)],
                                 T.t[:, 4 * CW * c:4 * CW * (c + 1)]).then_inc(S["q%d" % c], 1)
    for h in range(2):
        g.vector.wait_ge(S["wl%d" % h], 16)
        g.vector.quantize_mx(T.wq[:, 256 * h:256 * (h + 1)], T.ws[:, 256 * h:256 * (h + 1)],
                             T.wt[:, 1024 * h:1024 * (h + 1)]).then_inc(S["wq%d" % h], 1)

    for c in range(NP):
        g.tensor.wait_ge(S["arr%d" % c], 2 * k_in)
        for i in range(G):
            if c == 0 and i % 2 == 0:
                g.tensor.wait_ge(S["wq%d" % (i // 2)], 1)
            j = G * c + i
            g.tensor.matmul_mx(T.ps[:, BANK * j:BANK * j + CW],
                               T.wq[:, 128 * i:128 * (i + 1)], T.ws[:, 128 * i:128 * (i + 1)],
                               T.aq[:, CW * c:CW * (c + 1)], T.asc[:, CW * c:CW * (c + 1)], True, True).then_inc(S["mm%d" % j], 1)

    if not last:
        for c in range(NP):
            for i in range(G):
                j = G * c + i
                out = T.t[:, 4 * CW * c + i:4 * CW * (c + 1):4]
                z = T.ps[:, BANK * j:BANK * j + CW]
                if i % 2:
                    g.vector.wait_ge(S["mm%d" % j], 1)
                    g.vector.tensor_scalar(out, z, 0.0, SCALE, AluOpType.max, AluOpType.mult).then_inc(S["act%d" % c], 1)
                else:
                    g.scalar.wait_ge(S["mm%d" % j], 1)
                    g.scalar.activation(out, z, ActivationFunctionType.Relu, scale=SCALE).then_inc(S["act%d" % c], 1)
            g.vector.wait_ge(S["act%d" % c], G)
            g.vector.quantize_mx(T.hq[:, CW * c:CW * (c + 1)], T.hs[:, CW * c:CW * (c + 1)],
                                 T.t[:, 4 * CW * c:4 * CW * (c + 1)]).then_inc(S["q%d" % c], 1)
    else:
        for c in range(NP):
            for i in range(G):
                j = G * c + i
                a = NC * i + CW * c
                g.vector.wait_ge(S["mm%d" % j], 1)
                g.vector.tensor_copy(T.yt[:, a:a + CW], T.ps[:, BANK * j:BANK * j + CW]).then_inc(S["cp%d" % j], 1)
                q = ldq[i % 2]
                q.wait_ge(S["cp%d" % j], 1)
                q.dma_start(T.y[:, a:a + CW], T.yt[:, a:a + CW]).then_inc(S["st%d" % (i % 2)], 16)
        for h in range(2):
            ldq[h].wait_ge(S["st%d" % h], 16 * NP * G // 2)

    for c in range(NP):
        g.wait_ge(S["q%d" % c], 1)
        g.remote_dma(T.aq[:, CW * c:CW * (c + 1)].bitcast(dt.uint8), T.hq[:, CW * c:CW * (c + 1)].bitcast(dt.uint8),
                     S["arr%d" % c], S.sent, pid, rid, mask)
        g.remote_dma(T.asc[:, CW * c:CW * (c + 1)], T.hs[:, CW * c:CW * (c + 1)],
                     S["arr%d" % c], S.sent, pid, rid, mask)
    g.wait_ge(S.sent, 2 * NP * k_out)
